import numpy as np
import ml_dtypes


def mxq(x, axis, fmt="e4m3"):
    dtype, down = {"e4m3": (ml_dtypes.float8_e4m3fn, 7), "e5m2": (ml_dtypes.float8_e5m2, 14)}[fmt]
    v = np.moveaxis(np.asarray(x, np.float32).astype(ml_dtypes.bfloat16).astype(np.float64), axis, -1)
    blocks = v.reshape(v.shape[:-1] + (-1, 32))
    amax = np.abs(blocks).max(-1, keepdims=True)
    byte = np.maximum(np.where(amax > 0, np.frexp(amax)[1] - 1 + 127, 0) - down, 1)
    scale = np.exp2(byte - 127.0)
    codes = (blocks / scale).astype(np.float32).astype(dtype).astype(np.float64)
    return np.moveaxis((codes * scale).reshape(v.shape), -1, axis)


WIDE = False


def mx_kscale(k):
    if not WIDE:
        return np.ones(k)
    levels = np.array([30, -30])
    if k % 512:
        return np.exp2(np.random.permutation(np.resize(levels, k // 32))).repeat(32)
    a = np.empty((k // 512, 16))
    for p in range(k // 512):
        a[p, :8] = np.random.permutation(np.resize(levels, 8))
        for g in range(8):
            far = levels[np.abs(levels - a[p, g]) >= 10]
            a[p, g + 8] = far[np.random.randint(len(far))]
    return np.exp2(a.ravel()).repeat(32)


def f64(x):
    return np.asarray(x).astype(np.float64)


def striped(idx):
    return np.tile(np.asarray(idx).reshape(-1, 16).T, (8, 1)).astype(np.uint16)


def unstriped(offs):
    return offs[:16].T.reshape(-1).astype(np.int64)


E2M1 = np.array([0.0, 0.5, 1.0, 1.5, 2.0, 3.0, 4.0, 6.0, -0.0, -0.5, -1.0, -1.5, -2.0, -3.0, -4.0, -6.0])


def pack_weight(w, fmt):
    k, n = w.shape
    w = f64(np.asarray(w, np.float32).astype(ml_dtypes.bfloat16)).reshape(k // 32, 32, n)
    amax = np.abs(w).max(1)
    if fmt in ("e4m3", "e5m2"):
        byte = np.frexp(amax)[1] - 1 + 127 - (7 if fmt == "e4m3" else 14)
    else:
        mant, ex = np.frexp(amax / 6.0)
        byte = np.where(mant > 0.5, ex, ex - 1) + 127
    byte = np.clip(np.where(amax > 0, byte, 1), 1, 254)
    scaled = (w * np.exp2(127.0 - byte)[:, None, :]).reshape(k, n).astype(np.float32)
    by_word = np.ascontiguousarray(scaled.reshape(k // 512, 128, 4, n).transpose(0, 1, 3, 2))
    if fmt in ("e4m3", "e5m2"):
        words = by_word.astype(ml_dtypes.float8_e4m3fn if fmt == "e4m3" else ml_dtypes.float8_e5m2).view(np.uint8)
    else:
        c = by_word.astype(ml_dtypes.float4_e2m1fn).view(np.uint8) & 0xF
        words = (c[..., 0::2] | (c[..., 1::2] << 4)).reshape(k // 512, 128, 2 * n)
    return np.ascontiguousarray(words), np.ascontiguousarray(byte.astype(np.uint8).reshape(k // 512, 16, n))


def unpack_weight(words, scales, fmt):
    g, _, n = scales.shape
    words = np.ascontiguousarray(words).reshape(g, 128, n, -1)
    if fmt in ("e4m3", "e5m2"):
        vals = words.view(ml_dtypes.float8_e4m3fn if fmt == "e4m3" else ml_dtypes.float8_e5m2).astype(np.float64)
    else:
        nib = np.empty((g, 128, n, 4), np.uint8)
        nib[..., 0::2] = words & 0xF
        nib[..., 1::2] = words >> 4
        vals = E2M1[nib]
    vals = vals * np.repeat(np.exp2(scales.astype(np.float64) - 127.0), 8, axis=1)[..., None]
    return vals.transpose(0, 1, 3, 2).reshape(g * 512, n)


K, T, J, R, F, Z, O, N, L, E = 512, 1024, 256, 512, 512, 1024, 128, 256, 512, 512


def setup_inputs():
    n = np.random.standard_normal
    idx = np.random.permutation(T)[:J]
    idx2 = np.random.permutation(Z)[:J]
    idx3 = np.random.permutation(J)[:O]
    idx4 = np.random.permutation(J)[:O]
    idx5 = np.random.permutation(J)[:O]
    idx6 = np.random.permutation(E)[:O]
    idx7 = np.random.permutation(E)[:O]
    ff = mx_kscale(F)
    fk = mx_kscale(K)
    fr = mx_kscale(R)
    fl = mx_kscale(L)
    xop = pack_weight(n((F, Z)) / ff[:, None], "e2m1")
    wp = pack_weight(n((K, R)) * 1 / np.sqrt(K) / fk[:, None] * fr, "e2m1")
    w2p = pack_weight(n((F, R)) * 1 / np.sqrt(F) * ff[:, None], "e5m2")
    wbp = pack_weight(n((R, N)) * 1 / np.sqrt(R) / fr[:, None], "e5m2")
    sxp = pack_weight(n((L, O)) / fl[:, None], "e2m1")
    wsp = pack_weight(n((L, N)) * 1 / np.sqrt(L) * fl[:, None], "e5m2")
    return {
        "xo_words": xop[0],
        "xo_scales": xop[1],
        "cq": (np.random.randint(-7, 8, (K, T)).astype(np.float64)).astype(np.float32),
        "gs": (np.random.uniform(0.1, 0.4, (K, 1)) * fk[:, None]).astype(np.float32),
        "w_words": wp[0],
        "w_scales": wp[1],
        "w2_words": w2p[0],
        "w2_scales": w2p[1],
        "wb_words": wbp[0],
        "wb_scales": wbp[1],
        "sx_words": sxp[0],
        "sx_scales": sxp[1],
        "ws_words": wsp[0],
        "ws_scales": wsp[1],
        "offs": striped(idx),
        "offs2": striped(idx2),
        "offs3": striped(idx3),
        "offs4": striped(idx4),
        "offs5": striped(idx5),
        "offs6": striped(idx6),
        "offs7": striped(idx7),
    }


def reference(xo_words, xo_scales, cq, gs, w_words, w_scales, w2_words, w2_scales, wb_words, wb_scales, sx_words, sx_scales, ws_words, ws_scales, offs, offs2, offs3, offs4, offs5, offs6, offs7):
    idx = unstriped(offs)
    idx2 = unstriped(offs2)
    idx3 = unstriped(offs3)
    idx4 = unstriped(offs4)
    idx5 = unstriped(offs5)
    idx6 = unstriped(offs6)
    idx7 = unstriped(offs7)
    xou = unpack_weight(xo_words, xo_scales, "e2m1")
    wu = unpack_weight(w_words, w_scales, "e2m1")
    w2u = unpack_weight(w2_words, w2_scales, "e5m2")
    wbu = unpack_weight(wb_words, wb_scales, "e5m2")
    sxu = unpack_weight(sx_words, sx_scales, "e2m1")
    wsu = unpack_weight(ws_words, ws_scales, "e5m2")
    x1 = f64(cq)[:, idx] * f64(gs)
    x1q = mxq(x1, 0, "e4m3")
    a = wu.T @ x1q
    xoidx2g = xou[:, idx2]
    b = w2u.T @ xoidx2g
    lb = b[:, 0:1]
    la = a[:, 0:1]
    lb2 = b[:, 128:129]
    hid = np.maximum(a[:, idx3] * lb + b[:, idx4] * la + a[:, idx5] * lb2, 0.0)
    hidq = mxq(hid, 0, "e4m3")
    p = wbu.T @ hidq + wsu.T @ sxu
    pa = np.zeros((N, E))
    pa[:, idx6] = p
    pb = np.zeros((N, E))
    pb[:, idx7] = p
    y = pa + pb
    return y

@@ -1,0 +1,200 @@
+from contextlib import ExitStack
+
+import concourse.mybir as mybir
+
+K, T, J, R, F, Z, O, N, L, E = 512, 1024, 256, 512, 512, 1024, 128, 256, 512, 512
+FLOPS = 2 * (K * R * J + F * R * J + R * N * O + L * N * O)
+
+F32 = mybir.dt.float32
+BF16 = mybir.dt.bfloat16
+I32 = mybir.dt.int32
+U32 = mybir.dt.uint32
+U16 = mybir.dt.uint16
+U8 = mybir.dt.uint8
+E4M3 = mybir.dt.float8_e4m3fn_x4
+E5M2 = mybir.dt.float8_e5m2_x4
+E2M1 = mybir.dt.float4_e2m1fn_x4
+COPY = mybir.ActivationFunctionType.Copy
+ADD = mybir.AluOpType.add
+MAX = mybir.AluOpType.max
+
+P = 128
+PACK = 4
+QUAD = 32
+
+
+def staged_rows(scales):
+    return scales[0].bitcast(I32).rearrange("(q r) c -> r q c", r=PACK)
+
+
+def tile_list_leadsum_codednote_further_pagetwice_kernel(
+    tc, xo_words, xo_scales, cq, gs, w_words, w_scales, w2_words, w2_scales, wb_words, wb_scales,
+    sx_words, sx_scales, ws_words, ws_scales, offs, offs2, offs3, offs4, offs5, offs6, offs7, out,
+):
+    nc = tc.nc
+    with ExitStack() as ctx:
+        keep = ctx.enter_context(tc.tile_pool(name="keep", bufs=1))
+        psum = ctx.enter_context(tc.psum_pool(name="psum", bufs=1))
+
+        def load_list(name, src):
+            tile = keep.tile(list(src.shape), U16, name=name)
+            nc.sync.dma_start(tile[:], src)
+            return tile
+
+        def load_words(name, src, dtype, cols):
+            tile = keep.tile([P, cols], dtype, name=name, align_bytes=64)
+            nc.sync.dma_start(tile[:].bitcast(I32), src.bitcast(I32))
+            return tile
+
+        xo_stage = keep.tile([P, PACK, Z // 4], I32, name="xo_stage")
+        nc.vector.memset(xo_stage[2 * QUAD : 3 * QUAD], 0)
+        first_plane_raw = keep.tile([P, 2 * R], U8, name="first_plane_raw", align_bytes=64)
+        nc.vector.memset(first_plane_raw[:].bitcast(I32), 0)
+        second_plane = keep.tile([P, 2 * N + O], U8, name="second_plane", align_bytes=64)
+        nc.vector.memset(second_plane[:].bitcast(I32), 0)
+        pages = [[keep.tile([P, E], F32, name="page%d%d" % (h, s)) for s in range(2)] for h in range(N // P)]
+        for h in range(N // P):
+            for s in range(2):
+                nc.vector.memset(pages[h][s][:], 0.0)
+
+        cq_rows = cq.rearrange("(p t) c -> p t c", t=PACK)
+        cq_sb = [keep.tile([P, T], F32, name="cq%d" % t) for t in range(PACK)]
+        gs_sb = keep.tile([P, PACK], F32, name="gs_sb")
+        nc.sync.dma_start(cq_sb[0][:], cq_rows[:, 0, :])
+        nc.scalar.dma_start(gs_sb[:], gs.rearrange("(p t) o -> p (t o)", t=PACK))
+        l1 = load_list("l1", offs)
+        nc.sync.dma_start(cq_sb[1][:], cq_rows[:, 1, :])
+        l2 = load_list("l2", offs2)
+        nc.sync.dma_start(cq_sb[2][:], cq_rows[:, 2, :])
+        nc.sync.dma_start(cq_sb[3][:], cq_rows[:, 3, :])
+
+        first_stage = keep.tile([PACK, PACK, 2 * R // 4], I32, name="first_stage")
+        second_stage = keep.tile([PACK, PACK, (2 * N + O) // 4], I32, name="second_stage")
+        nc.scalar.dma_start(first_stage[:, :, 0 : R // 4], staged_rows(w_scales))
+        nc.scalar.dma_start(first_stage[:, :, R // 4 : 2 * R // 4], staged_rows(w2_scales))
+        nc.scalar.dma_start(xo_stage[2 * QUAD : 2 * QUAD + PACK], staged_rows(xo_scales))
+        nc.gpsimd.dma_start(second_stage[:, :, 0 : N // 4], staged_rows(wb_scales))
+        nc.gpsimd.dma_start(second_stage[:, :, N // 4 : 2 * N // 4], staged_rows(ws_scales))
+        nc.gpsimd.dma_start(second_stage[:, :, 2 * N // 4 :], staged_rows(sx_scales))
+
+        xo_w = load_words("xo_w", xo_words[0], U16, Z)
+        w_raw = load_words("w_raw", w_words[0], U16, R)
+        w2_raw = load_words("w2_raw", w2_words[0].rearrange("p n t -> p (n t)"), U32, R)
+        l3 = load_list("l3", offs3)
+        l5 = load_list("l5", offs5)
+        l4 = load_list("l4", offs4)
+        wb_w = load_words("wb_w", wb_words[0].rearrange("p n t -> p (n t)"), U32, N)
+        ws_w = load_words("ws_w", ws_words[0].rearrange("p n t -> p (n t)"), U32, N)
+        sx_w = load_words("sx_w", sx_words[0], U16, O)
+        l6 = load_list("l6", offs6)
+        l7 = load_list("l7", offs7)
+
+        for q in range(PACK):
+            nc.vector.tensor_copy(first_plane_raw[QUAD * q : QUAD * q + PACK].bitcast(I32), first_stage[:, q, :])
+        first_plane = keep.tile([P, 2, PACK, P], U8, name="first_plane", align_bytes=64)
+        nc.vector.tensor_copy(first_plane[:], first_plane_raw[:].rearrange("p (i m t) -> p i t m", i=2, t=PACK))
+        xo_plane = keep.tile([P, Z], U8, name="xo_plane", align_bytes=64)
+        for q in range(PACK):
+            nc.vector.tensor_copy(xo_plane[QUAD * q : QUAD * (q + 1)].bitcast(I32), xo_stage[2 * QUAD : 3 * QUAD, q, :])
+        xo_pick_s = keep.tile([P, J], U8, name="xo_pick_s", align_bytes=64)
+        nc.vector.tensor_copy(xo_pick_s[:], xo_plane[:].indirect(l2[:]))
+        for q in range(PACK):
+            nc.vector.tensor_copy(second_plane[QUAD * q : QUAD * q + PACK].bitcast(I32), second_stage[:, q, :])
+
+        x1_rows = keep.tile([P, PACK, J], BF16, name="x1_rows")
+        for t in range(PACK):
+            nc.scalar.activation(x1_rows[:, t, :], cq_sb[t][:].indirect(l1[:]), COPY, scale=gs_sb[:, t : t + 1])
+        x1_grouped = keep.tile([P, J, PACK], BF16, name="x1_grouped", align_bytes=64)
+        nc.vector.tensor_copy(
+            x1_grouped[:].rearrange("p (c i) t -> p c t i", i=4), x1_rows[:].rearrange("p t (c i) -> p c t i", i=4)
+        )
+        xo_pick_w = keep.tile([P, J], U16, name="xo_pick_w", align_bytes=64)
+        nc.vector.tensor_copy(xo_pick_w[:], xo_w[:].indirect(l2[:]))
+        x1_codes = keep.tile([P, J], U32, name="x1_codes", align_bytes=64)
+        x1_plane = keep.tile([P, J], U8, name="x1_plane", align_bytes=64)
+        nc.vector.quantize_mx(x1_codes[:].bitcast(E4M3), x1_plane[:], x1_grouped[:].rearrange("p j t -> p (j t)"))
+
+        w_w = keep.tile([P, PACK, P], U16, name="w_w", align_bytes=64)
+        nc.scalar.copy(w_w[:], w_raw[:].rearrange("p (m t) -> p t m", t=PACK))
+        w2_w = keep.tile([P, PACK, P], U32, name="w2_w", align_bytes=64)
+        nc.scalar.copy(w2_w[:].rearrange("p t m -> p m t"), w2_raw[:].rearrange("p (m t) -> p m t", t=PACK))
+
+        p_ps = [psum.tile([P, O], F32, name="p_ps%d" % h) for h in range(N // P)]
+
+        picks = keep.tile([P, 3, PACK, O], F32, name="picks")
+        part = keep.tile([P, PACK, O], F32, name="part")
+        total = keep.tile([P, PACK, O], F32, name="total")
+        a_sb, b_sb = [], []
+        for t in range(PACK):
+            b_ps = psum.tile([P, J], F32, name="b_ps", tag="ab", bufs=6)
+            nc.tensor.matmul_mx(
+                b_ps[:], lhsT=w2_w[:, t, :].bitcast(E5M2), lhsT_scale=first_plane[:, 1, t, :],
+                rhs=xo_pick_w[:].bitcast(E2M1), rhs_scale=xo_pick_s[:], start=True, stop=True,
+            )
+            a_ps = psum.tile([P, J], F32, name="a_ps", tag="ab", bufs=6)
+            nc.tensor.matmul_mx(
+                a_ps[:], lhsT=w_w[:, t, :].bitcast(E2M1), lhsT_scale=first_plane[:, 0, t, :],
+                rhs=x1_codes[:].bitcast(E4M3), rhs_scale=x1_plane[:], start=True, stop=True,
+            )
+            b_t = keep.tile([P, J], F32, name="b%d" % t)
+            a_t = keep.tile([P, J], F32, name="a%d" % t)
+            if t == 0:
+                nc.scalar.copy(b_t[:], b_ps[:])
+            else:
+                nc.vector.tensor_copy(b_t[:], b_ps[:])
+            nc.vector.tensor_copy(a_t[:], a_ps[:])
+            a_sb.append(a_t)
+            b_sb.append(b_t)
+
+        for h in range(N // P):
+            nc.tensor.matmul_mx(
+                p_ps[h][:],
+                lhsT=ws_w[:, P * h : P * (h + 1)].bitcast(E5M2),
+                lhsT_scale=second_plane[:, N + P * h : N + P * (h + 1)],
+                rhs=sx_w[:].bitcast(E2M1),
+                rhs_scale=second_plane[:, 2 * N :],
+                start=True,
+                stop=False,
+            )
+
+        for t in range(PACK):
+            nc.scalar.activation(picks[:, 0, t, :], a_sb[t][:].indirect(l3[:]), COPY, scale=b_sb[t][:, 0:1])
+            nc.scalar.activation(picks[:, 1, t, :], a_sb[t][:].indirect(l5[:]), COPY, scale=b_sb[t][:, 128:129])
+            nc.scalar.activation(picks[:, 2, t, :], b_sb[t][:].indirect(l4[:]), COPY, scale=a_sb[t][:, 0:1])
+            nc.vector.tensor_tensor(part[:, t, :], picks[:, 0, t, :], picks[:, 1, t, :], ADD)
+            nc.vector.tensor_tensor(total[:, t, :], part[:, t, :], picks[:, 2, t, :], ADD)
+
+        hid_grouped = keep.tile([P, O, PACK], BF16, name="hid_grouped", align_bytes=64)
+        nc.vector.tensor_scalar(
+            hid_grouped[:].rearrange("p (c i) t -> p c t i", i=4),
+            total[:].rearrange("p t (c i) -> p c t i", i=4),
+            0.0, None, MAX,
+        )
+        hid_codes = keep.tile([P, O], U32, name="hid_codes", align_bytes=64)
+        hid_plane = keep.tile([P, O], U8, name="hid_plane", align_bytes=64)
+        nc.vector.quantize_mx(hid_codes[:].bitcast(E4M3), hid_plane[:], hid_grouped[:].rearrange("p o t -> p (o t)"))
+
+        p_sb = []
+        for h in range(N // P):
+            nc.tensor.matmul_mx(
+                p_ps[h][:],
+                lhsT=wb_w[:, P * h : P * (h + 1)].bitcast(E5M2),
+                lhsT_scale=second_plane[:, P * h : P * (h + 1)],
+                rhs=hid_codes[:].bitcast(E4M3),
+                rhs_scale=hid_plane[:],
+                start=False,
+                stop=True,
+            )
+            p_h = keep.tile([P, O], F32, name="p%d" % h)
+            if h == 0:
+                nc.vector.tensor_copy(p_h[:], p_ps[h][:])
+            else:
+                nc.scalar.copy(p_h[:], p_ps[h][:])
+            p_sb.append(p_h)
+        for h in range(N // P):
+            nc.vector.tensor_copy(pages[h][0][:].indirect(l6[:]), p_sb[h][:])
+            nc.scalar.activation(pages[h][1][:].indirect(l7[:]), p_sb[h][:], COPY)
+        for h in range(N // P):
+            both = keep.tile([P, E], F32, name="both%d" % h)
+            nc.vector.tensor_tensor(both[:], pages[h][0][:], pages[h][1][:], ADD)
+            nc.sync.dma_start(out[P * h : P * (h + 1), :], both[:])

@@ -42,88 +42,95 @@ def tile_list_leadsum_codednote_further_pagetwice_kernel(
             return tile
 
         def load_words(name, src, dtype, cols):
-            tile = keep.tile([P, cols], dtype, name=name, align_bytes=64)
+            tile = keep.tile([P, cols], dtype, name=name, tag=name, align_bytes=64)
             nc.sync.dma_start(tile[:].bitcast(I32), src.bitcast(I32))
             return tile
 
-        xo_stage = keep.tile([P, PACK, Z // 4], I32, name="xo_stage")
-        nc.vector.memset(xo_stage[2 * QUAD : 3 * QUAD], 0)
-        first_plane_raw = keep.tile([P, 2 * R], U8, name="first_plane_raw", align_bytes=64)
+        xo_plane = keep.tile([P, Z], U8, name="xo_plane", align_bytes=64)
+        nc.vector.memset(xo_plane[:].bitcast(I32), 0)
+        first_plane_raw = keep.tile([P, 2 * R], U8, name="first_plane_raw", tag="x1_grouped", align_bytes=64)
         nc.vector.memset(first_plane_raw[:].bitcast(I32), 0)
-        second_plane = keep.tile([P, 2 * N + O], U8, name="second_plane", align_bytes=64)
-        nc.vector.memset(second_plane[:].bitcast(I32), 0)
-        pages = [[keep.tile([P, E], F32, name="page%d%d" % (h, s)) for s in range(2)] for h in range(N // P)]
-        for h in range(N // P):
-            for s in range(2):
-                nc.vector.memset(pages[h][s][:], 0.0)
+        second_stage = keep.tile([QUAD, PACK, (2 * N + O) // 4], I32, name="second_stage")
+        nc.vector.memset(second_stage[:], 0)
 
         cq_rows = cq.rearrange("(p t) c -> p t c", t=PACK)
-        cq_sb = [keep.tile([P, T], F32, name="cq%d" % t) for t in range(PACK)]
+        cq_sb = [keep.tile([P, T], F32, name="cq%d" % t, tag="cq%d" % t, align_bytes=64) for t in range(PACK)]
         gs_sb = keep.tile([P, PACK], F32, name="gs_sb")
-        nc.sync.dma_start(cq_sb[0][:], cq_rows[:, 0, :])
+        xo_stage = keep.tile([P, 2, Z // 4], I32, name="xo_stage")
+        first_stage = keep.tile([P, 2, 2 * R // 4], I32, name="first_stage")
+        for stage, scales, cols in (
+            (xo_stage, xo_scales, slice(0, Z // 4)),
+            (first_stage, w_scales, slice(0, R // 4)),
+            (first_stage, w2_scales, slice(R // 4, 2 * R // 4)),
+        ):
+            for half in range(2):
+                nc.scalar.dma_start(
+                    stage[2 * QUAD * half : 2 * QUAD * half + PACK, :, cols],
+                    staged_rows(scales)[:, 2 * half : 2 * half + 2, :],
+                )
         nc.scalar.dma_start(gs_sb[:], gs.rearrange("(p t) o -> p (t o)", t=PACK))
         l1 = load_list("l1", offs)
-        nc.sync.dma_start(cq_sb[1][:], cq_rows[:, 1, :])
+        nc.sync.dma_start(cq_sb[0][:], cq_rows[:, 0, :])
         l2 = load_list("l2", offs2)
-        nc.sync.dma_start(cq_sb[2][:], cq_rows[:, 2, :])
-        nc.sync.dma_start(cq_sb[3][:], cq_rows[:, 3, :])
-
-        first_stage = keep.tile([PACK, PACK, 2 * R // 4], I32, name="first_stage")
-        second_stage = keep.tile([PACK, PACK, (2 * N + O) // 4], I32, name="second_stage")
-        nc.scalar.dma_start(first_stage[:, :, 0 : R // 4], staged_rows(w_scales))
-        nc.scalar.dma_start(first_stage[:, :, R // 4 : 2 * R // 4], staged_rows(w2_scales))
-        nc.scalar.dma_start(xo_stage[2 * QUAD : 2 * QUAD + PACK], staged_rows(xo_scales))
-        nc.gpsimd.dma_start(second_stage[:, :, 0 : N // 4], staged_rows(wb_scales))
-        nc.gpsimd.dma_start(second_stage[:, :, N // 4 : 2 * N // 4], staged_rows(ws_scales))
-        nc.gpsimd.dma_start(second_stage[:, :, 2 * N // 4 :], staged_rows(sx_scales))
-
+        for t in range(1, PACK):
+            nc.sync.dma_start(cq_sb[t][:], cq_rows[:, t, :])
         xo_w = load_words("xo_w", xo_words[0], U16, Z)
-        w_raw = load_words("w_raw", w_words[0], U16, R)
         w2_raw = load_words("w2_raw", w2_words[0].rearrange("p n t -> p (n t)"), U32, R)
+        w_raw = load_words("w_raw", w_words[0], U16, R)
         l3 = load_list("l3", offs3)
         l5 = load_list("l5", offs5)
         l4 = load_list("l4", offs4)
+        nc.sync.dma_start(second_stage[0:PACK, :, 0 : N // 4], staged_rows(wb_scales))
+        nc.sync.dma_start(second_stage[0:PACK, :, N // 4 : 2 * N // 4], staged_rows(ws_scales))
+        nc.sync.dma_start(second_stage[0:PACK, :, 2 * N // 4 :], staged_rows(sx_scales))
         wb_w = load_words("wb_w", wb_words[0].rearrange("p n t -> p (n t)"), U32, N)
         ws_w = load_words("ws_w", ws_words[0].rearrange("p n t -> p (n t)"), U32, N)
         sx_w = load_words("sx_w", sx_words[0], U16, O)
         l6 = load_list("l6", offs6)
         l7 = load_list("l7", offs7)
 
-        for q in range(PACK):
-            nc.vector.tensor_copy(first_plane_raw[QUAD * q : QUAD * q + PACK].bitcast(I32), first_stage[:, q, :])
-        first_plane = keep.tile([P, 2, PACK, P], U8, name="first_plane", align_bytes=64)
-        nc.vector.tensor_copy(first_plane[:], first_plane_raw[:].rearrange("p (i m t) -> p i t m", i=2, t=PACK))
-        xo_plane = keep.tile([P, Z], U8, name="xo_plane", align_bytes=64)
-        for q in range(PACK):
-            nc.vector.tensor_copy(xo_plane[QUAD * q : QUAD * (q + 1)].bitcast(I32), xo_stage[2 * QUAD : 3 * QUAD, q, :])
+        def spread(plane, stage):
+            for q in range(PACK):
+                src = 2 * QUAD * (q // 2)
+                nc.vector.tensor_copy(plane[QUAD * q : QUAD * q + PACK].bitcast(I32), stage[src : src + PACK, q % 2, :])
+
+        spread(xo_plane, xo_stage)
         xo_pick_s = keep.tile([P, J], U8, name="xo_pick_s", align_bytes=64)
         nc.vector.tensor_copy(xo_pick_s[:], xo_plane[:].indirect(l2[:]))
-        for q in range(PACK):
-            nc.vector.tensor_copy(second_plane[QUAD * q : QUAD * q + PACK].bitcast(I32), second_stage[:, q, :])
+        spread(first_plane_raw, first_stage)
+        first_plane = keep.tile([P, 2, PACK, P], U8, name="first_plane", align_bytes=64)
+        nc.vector.tensor_copy(first_plane[:], first_plane_raw[:].rearrange("p (i m t) -> p i t m", i=2, t=PACK))
 
-        x1_rows = keep.tile([P, PACK, J], BF16, name="x1_rows")
+        x1_grouped = keep.tile([P, J, PACK], BF16, name="x1_grouped", tag="x1_grouped", align_bytes=64)
+        x1_early = keep.tile([P, 2, J], BF16, name="x1_early")
+        x1_late = keep.tile([P, 2, J], BF16, name="x1_late", tag="x1_late", align_bytes=64)
         for t in range(PACK):
-            nc.scalar.activation(x1_rows[:, t, :], cq_sb[t][:].indirect(l1[:]), COPY, scale=gs_sb[:, t : t + 1])
-        x1_grouped = keep.tile([P, J, PACK], BF16, name="x1_grouped", align_bytes=64)
-        nc.vector.tensor_copy(
-            x1_grouped[:].rearrange("p (c i) t -> p c t i", i=4), x1_rows[:].rearrange("p t (c i) -> p c t i", i=4)
-        )
-        xo_pick_w = keep.tile([P, J], U16, name="xo_pick_w", align_bytes=64)
+            row = x1_early[:, t, :] if t < 2 else x1_late[:, t - 2, :]
+            nc.scalar.activation(row, cq_sb[t][:].indirect(l1[:]), COPY, scale=gs_sb[:, t : t + 1])
+        nc.vector.tensor_copy(x1_grouped[:, :, 0:2], x1_early[:].rearrange("p t j -> p j t"))
+        nc.vector.tensor_copy(x1_grouped[:, :, 2:4], x1_late[:].rearrange("p t j -> p j t"))
+        xo_pick_w = keep.tile([P, J], U16, name="xo_pick_w", tag="x1_late", align_bytes=64)
         nc.vector.tensor_copy(xo_pick_w[:], xo_w[:].indirect(l2[:]))
-        x1_codes = keep.tile([P, J], U32, name="x1_codes", align_bytes=64)
+        x1_codes = keep.tile([P, J], U32, name="x1_codes", tag="codes_then_plane", align_bytes=64)
         x1_plane = keep.tile([P, J], U8, name="x1_plane", align_bytes=64)
         nc.vector.quantize_mx(x1_codes[:].bitcast(E4M3), x1_plane[:], x1_grouped[:].rearrange("p j t -> p (j t)"))
 
-        w_w = keep.tile([P, PACK, P], U16, name="w_w", align_bytes=64)
-        nc.scalar.copy(w_w[:], w_raw[:].rearrange("p (m t) -> p t m", t=PACK))
-        w2_w = keep.tile([P, PACK, P], U32, name="w2_w", align_bytes=64)
-        nc.scalar.copy(w2_w[:].rearrange("p t m -> p m t"), w2_raw[:].rearrange("p (m t) -> p m t", t=PACK))
+        dealt = keep.tile([P, R + R // 2], U32, name="dealt", tag="cq3", align_bytes=64)
+        w2_w = dealt[:, 0:R].rearrange("p (t m) -> p t m", t=PACK)
+        w_w = dealt[:, R:].bitcast(U16).rearrange("p (t m) -> p t m", t=PACK)
+        w2_cols = w2_raw[:].rearrange("p (m t) -> p m t", t=PACK)
+        w_cols = w_raw[:].rearrange("p (m t) -> p t m", t=PACK)
+        nc.scalar.copy(w2_w[:, 0, :], w2_cols[:, :, 0])
+        nc.scalar.copy(w_w[:, 0, :], w_cols[:, 0, :])
+        nc.scalar.copy(w2_w[:, 1:, :].rearrange("p t m -> p m t"), w2_cols[:, :, 1:])
+        nc.scalar.copy(w_w[:, 1:, :], w_cols[:, 1:, :])
 
         p_ps = [psum.tile([P, O], F32, name="p_ps%d" % h) for h in range(N // P)]
 
         picks = keep.tile([P, 3, PACK, O], F32, name="picks")
         part = keep.tile([P, PACK, O], F32, name="part")
-        total = keep.tile([P, PACK, O], F32, name="total")
+        total = keep.tile([P, PACK - 1, O], F32, name="total")
+        total_last = keep.tile([P, O], F32, name="total_last")
         a_sb, b_sb = [], []
         for t in range(PACK):
             b_ps = psum.tile([P, J], F32, name="b_ps", tag="ab", bufs=6)
@@ -138,14 +145,14 @@ def tile_list_leadsum_codednote_further_pagetwice_kernel(
             )
             b_t = keep.tile([P, J], F32, name="b%d" % t)
             a_t = keep.tile([P, J], F32, name="a%d" % t)
-            if t == 0:
-                nc.scalar.copy(b_t[:], b_ps[:])
-            else:
-                nc.vector.tensor_copy(b_t[:], b_ps[:])
+            nc.vector.tensor_copy(b_t[:], b_ps[:])
             nc.vector.tensor_copy(a_t[:], a_ps[:])
             a_sb.append(a_t)
             b_sb.append(b_t)
 
+        second_plane = keep.tile([P, 2 * N + O], U8, name="second_plane", tag="codes_then_plane", align_bytes=64)
+        for q in range(PACK):
+            nc.vector.tensor_copy(second_plane[QUAD * q : QUAD * (q + 1)].bitcast(I32), second_stage[:, q, :])
         for h in range(N // P):
             nc.tensor.matmul_mx(
                 p_ps[h][:],
@@ -162,14 +169,22 @@ def tile_list_leadsum_codednote_further_pagetwice_kernel(
             nc.scalar.activation(picks[:, 1, t, :], a_sb[t][:].indirect(l5[:]), COPY, scale=b_sb[t][:, 128:129])
             nc.scalar.activation(picks[:, 2, t, :], b_sb[t][:].indirect(l4[:]), COPY, scale=a_sb[t][:, 0:1])
             nc.vector.tensor_tensor(part[:, t, :], picks[:, 0, t, :], picks[:, 1, t, :], ADD)
-            nc.vector.tensor_tensor(total[:, t, :], part[:, t, :], picks[:, 2, t, :], ADD)
+            nc.vector.tensor_tensor(total[:, t, :] if t < PACK - 1 else total_last[:], part[:, t, :], picks[:, 2, t, :], ADD)
+
+        page_tags = (("x1_grouped", "w2_raw"), ("w_raw", "x1_late"))
+        pages = [
+            [keep.tile([P, E], F32, name="page%d%d" % (h, s), tag=page_tags[h][s], align_bytes=64) for s in range(2)]
+            for h in range(N // P)
+        ]
+        for h in range(N // P):
+            for s in range(2):
+                nc.gpsimd.memset(pages[h][s][:], 0.0)
 
         hid_grouped = keep.tile([P, O, PACK], BF16, name="hid_grouped", align_bytes=64)
         nc.vector.tensor_scalar(
-            hid_grouped[:].rearrange("p (c i) t -> p c t i", i=4),
-            total[:].rearrange("p t (c i) -> p c t i", i=4),
-            0.0, None, MAX,
+            hid_grouped[:, :, 0 : PACK - 1], total[:, 0 : PACK - 1, :].rearrange("p t o -> p o t"), 0.0, None, MAX
         )
+        nc.vector.tensor_scalar(hid_grouped[:, :, PACK - 1], total_last[:], 0.0, None, MAX)
         hid_codes = keep.tile([P, O], U32, name="hid_codes", align_bytes=64)
         hid_plane = keep.tile([P, O], U8, name="hid_plane", align_bytes=64)
         nc.vector.quantize_mx(hid_codes[:].bitcast(E4M3), hid_plane[:], hid_grouped[:].rearrange("p o t -> p (o t)"))
@@ -194,7 +209,7 @@ def tile_list_leadsum_codednote_further_pagetwice_kernel(
         for h in range(N // P):
             nc.vector.tensor_copy(pages[h][0][:].indirect(l6[:]), p_sb[h][:])
             nc.scalar.activation(pages[h][1][:].indirect(l7[:]), p_sb[h][:], COPY)
-        for h in range(N // P):
-            both = keep.tile([P, E], F32, name="both%d" % h)
-            nc.vector.tensor_tensor(both[:], pages[h][0][:], pages[h][1][:], ADD)
-            nc.sync.dma_start(out[P * h : P * (h + 1), :], both[:])
+        for h, cols in ((0, slice(0, E)), (1, slice(0, E // 2)), (1, slice(E // 2, E))):
+            both = keep.tile([P, cols.stop - cols.start], F32, name="both%d_%d" % (h, cols.start))
+            nc.vector.tensor_tensor(both[:], pages[h][0][:, cols], pages[h][1][:, cols], ADD)
+            nc.sync.dma_start(out[P * h : P * (h + 1), cols], both[:])

@@ -34,6 +34,7 @@ def tile_list_leadsum_codednote_further_pagetwice_kernel(
     nc = tc.nc
     with ExitStack() as ctx:
         keep = ctx.enter_context(tc.tile_pool(name="keep", bufs=1))
+        shared = ctx.enter_context(tc.tile_pool(name="shared", bufs=1))
         psum = ctx.enter_context(tc.psum_pool(name="psum", bufs=1))
 
         def load_list(name, src):
@@ -46,15 +47,16 @@ def tile_list_leadsum_codednote_further_pagetwice_kernel(
             nc.sync.dma_start(tile[:].bitcast(I32), src.bitcast(I32))
             return tile
 
-        xo_plane = keep.tile([P, Z], U8, name="xo_plane", align_bytes=64)
+        xo_plane = keep.tile([P, Z], U8, name="xo_plane", tag="x1_grouped", align_bytes=64)
         nc.vector.memset(xo_plane[:].bitcast(I32), 0)
-        first_plane_raw = keep.tile([P, 2 * R], U8, name="first_plane_raw", tag="x1_grouped", align_bytes=64)
+        first_plane_raw = keep.tile([P, 2 * R], U8, name="first_plane_raw", align_bytes=64)
         nc.vector.memset(first_plane_raw[:].bitcast(I32), 0)
         second_stage = keep.tile([QUAD, PACK, (2 * N + O) // 4], I32, name="second_stage")
         nc.vector.memset(second_stage[:], 0)
 
         cq_rows = cq.rearrange("(p t) c -> p t c", t=PACK)
-        cq_sb = [keep.tile([P, T], F32, name="cq%d" % t, tag="cq%d" % t, align_bytes=64) for t in range(PACK)]
+        cq_sb = [keep.tile([P, T], F32, name="cq%d" % t) for t in range(PACK - 1)]
+        cq_sb.append(shared.tile([P, T], F32, name="cq_last", offset=0, align_bytes=64))
         gs_sb = keep.tile([P, PACK], F32, name="gs_sb")
         xo_stage = keep.tile([P, 2, Z // 4], I32, name="xo_stage")
         first_stage = keep.tile([P, 2, 2 * R // 4], I32, name="first_stage")
@@ -64,15 +66,16 @@ def tile_list_leadsum_codednote_further_pagetwice_kernel(
             (first_stage, w2_scales, slice(R // 4, 2 * R // 4)),
         ):
             for half in range(2):
-                nc.scalar.dma_start(
+                (nc.sync, nc.scalar)[half].dma_start(
                     stage[2 * QUAD * half : 2 * QUAD * half + PACK, :, cols],
                     staged_rows(scales)[:, 2 * half : 2 * half + 2, :],
                 )
         nc.scalar.dma_start(gs_sb[:], gs.rearrange("(p t) o -> p (t o)", t=PACK))
-        l1 = load_list("l1", offs)
-        nc.sync.dma_start(cq_sb[0][:], cq_rows[:, 0, :])
+        for t in range(2):
+            nc.sync.dma_start(cq_sb[t][:], cq_rows[:, t, :])
         l2 = load_list("l2", offs2)
-        for t in range(1, PACK):
+        l1 = load_list("l1", offs)
+        for t in range(2, PACK):
             nc.sync.dma_start(cq_sb[t][:], cq_rows[:, t, :])
         xo_w = load_words("xo_w", xo_words[0], U16, Z)
         w2_raw = load_words("w2_raw", w2_words[0].rearrange("p n t -> p (n t)"), U32, R)
@@ -95,11 +98,11 @@ def tile_list_leadsum_codednote_further_pagetwice_kernel(
                 nc.vector.tensor_copy(plane[QUAD * q : QUAD * q + PACK].bitcast(I32), stage[src : src + PACK, q % 2, :])
 
         spread(xo_plane, xo_stage)
-        xo_pick_s = keep.tile([P, J], U8, name="xo_pick_s", align_bytes=64)
-        nc.vector.tensor_copy(xo_pick_s[:], xo_plane[:].indirect(l2[:]))
         spread(first_plane_raw, first_stage)
         first_plane = keep.tile([P, 2, PACK, P], U8, name="first_plane", align_bytes=64)
         nc.vector.tensor_copy(first_plane[:], first_plane_raw[:].rearrange("p (i m t) -> p i t m", i=2, t=PACK))
+        xo_pick_s = keep.tile([P, J], U8, name="xo_pick_s", align_bytes=64)
+        nc.vector.tensor_copy(xo_pick_s[:], xo_plane[:].indirect(l2[:]))
 
         x1_grouped = keep.tile([P, J, PACK], BF16, name="x1_grouped", tag="x1_grouped", align_bytes=64)
         x1_early = keep.tile([P, 2, J], BF16, name="x1_early")
@@ -111,19 +114,22 @@ def tile_list_leadsum_codednote_further_pagetwice_kernel(
         nc.vector.tensor_copy(x1_grouped[:, :, 2:4], x1_late[:].rearrange("p t j -> p j t"))
         xo_pick_w = keep.tile([P, J], U16, name="xo_pick_w", tag="x1_late", align_bytes=64)
         nc.vector.tensor_copy(xo_pick_w[:], xo_w[:].indirect(l2[:]))
-        x1_codes = keep.tile([P, J], U32, name="x1_codes", tag="codes_then_plane", align_bytes=64)
+        x1_codes = keep.tile([P, J], U32, name="x1_codes", tag="xo_w", align_bytes=64)
         x1_plane = keep.tile([P, J], U8, name="x1_plane", align_bytes=64)
         nc.vector.quantize_mx(x1_codes[:].bitcast(E4M3), x1_plane[:], x1_grouped[:].rearrange("p j t -> p (j t)"))
 
-        dealt = keep.tile([P, R + R // 2], U32, name="dealt", tag="cq3", align_bytes=64)
-        w2_w = dealt[:, 0:R].rearrange("p (t m) -> p t m", t=PACK)
-        w_w = dealt[:, R:].bitcast(U16).rearrange("p (t m) -> p t m", t=PACK)
+        w2_first = shared.tile([P, P], U32, name="w2_first", offset=0, align_bytes=64)
+        w_first = shared.tile([P, P], U16, name="w_first", offset=4 * P, align_bytes=64)
+        w2_rest = shared.tile([P, PACK - 1, P], U32, name="w2_rest", offset=6 * P, align_bytes=64)
+        w_rest = shared.tile([P, PACK - 1, P], U16, name="w_rest", offset=18 * P, align_bytes=64)
         w2_cols = w2_raw[:].rearrange("p (m t) -> p m t", t=PACK)
         w_cols = w_raw[:].rearrange("p (m t) -> p t m", t=PACK)
-        nc.scalar.copy(w2_w[:, 0, :], w2_cols[:, :, 0])
-        nc.scalar.copy(w_w[:, 0, :], w_cols[:, 0, :])
-        nc.scalar.copy(w2_w[:, 1:, :].rearrange("p t m -> p m t"), w2_cols[:, :, 1:])
-        nc.scalar.copy(w_w[:, 1:, :], w_cols[:, 1:, :])
+        nc.scalar.copy(w2_first[:], w2_cols[:, :, 0])
+        nc.scalar.copy(w_first[:], w_cols[:, 0, :])
+        nc.scalar.copy(w2_rest[:].rearrange("p t m -> p m t"), w2_cols[:, :, 1:])
+        nc.scalar.copy(w_rest[:], w_cols[:, 1:, :])
+        w2_w = [w2_first[:]] + [w2_rest[:, t, :] for t in range(PACK - 1)]
+        w_w = [w_first[:]] + [w_rest[:, t, :] for t in range(PACK - 1)]
 
         p_ps = [psum.tile([P, O], F32, name="p_ps%d" % h) for h in range(N // P)]
 
@@ -135,12 +141,12 @@ def tile_list_leadsum_codednote_further_pagetwice_kernel(
         for t in range(PACK):
             b_ps = psum.tile([P, J], F32, name="b_ps", tag="ab", bufs=6)
             nc.tensor.matmul_mx(
-                b_ps[:], lhsT=w2_w[:, t, :].bitcast(E5M2), lhsT_scale=first_plane[:, 1, t, :],
+                b_ps[:], lhsT=w2_w[t].bitcast(E5M2), lhsT_scale=first_plane[:, 1, t, :],
                 rhs=xo_pick_w[:].bitcast(E2M1), rhs_scale=xo_pick_s[:], start=True, stop=True,
             )
             a_ps = psum.tile([P, J], F32, name="a_ps", tag="ab", bufs=6)
             nc.tensor.matmul_mx(
-                a_ps[:], lhsT=w_w[:, t, :].bitcast(E2M1), lhsT_scale=first_plane[:, 0, t, :],
+                a_ps[:], lhsT=w_w[t].bitcast(E2M1), lhsT_scale=first_plane[:, 0, t, :],
                 rhs=x1_codes[:].bitcast(E4M3), rhs_scale=x1_plane[:], start=True, stop=True,
             )
             b_t = keep.tile([P, J], F32, name="b%d" % t)
@@ -150,7 +156,7 @@ def tile_list_leadsum_codednote_further_pagetwice_kernel(
             a_sb.append(a_t)
             b_sb.append(b_t)
 
-        second_plane = keep.tile([P, 2 * N + O], U8, name="second_plane", tag="codes_then_plane", align_bytes=64)
+        second_plane = keep.tile([P, 2 * N + O], U8, name="second_plane", tag="xo_w", align_bytes=64)
         for q in range(PACK):
             nc.vector.tensor_copy(second_plane[QUAD * q : QUAD * (q + 1)].bitcast(I32), second_stage[:, q, :])
         for h in range(N // P):
@@ -189,7 +195,6 @@ def tile_list_leadsum_codednote_further_pagetwice_kernel(
         hid_plane = keep.tile([P, O], U8, name="hid_plane", align_bytes=64)
         nc.vector.quantize_mx(hid_codes[:].bitcast(E4M3), hid_plane[:], hid_grouped[:].rearrange("p o t -> p (o t)"))
 
-        p_sb = []
         for h in range(N // P):
             nc.tensor.matmul_mx(
                 p_ps[h][:],
@@ -200,16 +205,18 @@ def tile_list_leadsum_codednote_further_pagetwice_kernel(
                 start=False,
                 stop=True,
             )
-            p_h = keep.tile([P, O], F32, name="p%d" % h)
-            if h == 0:
-                nc.vector.tensor_copy(p_h[:], p_ps[h][:])
-            else:
-                nc.scalar.copy(p_h[:], p_ps[h][:])
-            p_sb.append(p_h)
-        for h in range(N // P):
-            nc.vector.tensor_copy(pages[h][0][:].indirect(l6[:]), p_sb[h][:])
-            nc.scalar.activation(pages[h][1][:].indirect(l7[:]), p_sb[h][:], COPY)
-        for h, cols in ((0, slice(0, E)), (1, slice(0, E // 2)), (1, slice(E // 2, E))):
+
+        def add_and_store(h, cols):
             both = keep.tile([P, cols.stop - cols.start], F32, name="both%d_%d" % (h, cols.start))
             nc.vector.tensor_tensor(both[:], pages[h][0][:, cols], pages[h][1][:, cols], ADD)
             nc.sync.dma_start(out[P * h : P * (h + 1), cols], both[:])
+
+        for h, empty_bank in enumerate((nc.vector.tensor_copy, nc.scalar.copy)):
+            p_sb = keep.tile([P, O], F32, name="p%d" % h, tag="p_sb")
+            empty_bank(p_sb[:], p_ps[h][:])
+            nc.vector.tensor_copy(pages[h][0][:].indirect(l6[:]), p_sb[:])
+            nc.scalar.activation(pages[h][1][:].indirect(l7[:]), p_sb[:], COPY)
+            if h == 0:
+                add_and_store(0, slice(0, E))
+        add_and_store(1, slice(0, E // 2))
+        add_and_store(1, slice(E // 2, E))

@@ -51,8 +51,8 @@ def tile_list_leadsum_codednote_further_pagetwice_kernel(
         nc.vector.memset(xo_plane[:].bitcast(I32), 0)
         first_plane_raw = keep.tile([P, 2 * R], U8, name="first_plane_raw", align_bytes=64)
         nc.vector.memset(first_plane_raw[:].bitcast(I32), 0)
-        second_stage = keep.tile([QUAD, PACK, (2 * N + O) // 4], I32, name="second_stage")
-        nc.vector.memset(second_stage[:], 0)
+        second_plane = keep.tile([P, 2 * N + O], U8, name="second_plane", align_bytes=64)
+        nc.vector.memset(second_plane[:].bitcast(I32), 0)
 
         cq_rows = cq.rearrange("(p t) c -> p t c", t=PACK)
         cq_sb = [keep.tile([P, T], F32, name="cq%d" % t) for t in range(PACK - 1)]
@@ -60,21 +60,21 @@ def tile_list_leadsum_codednote_further_pagetwice_kernel(
         gs_sb = keep.tile([P, PACK], F32, name="gs_sb")
         xo_stage = keep.tile([P, 2, Z // 4], I32, name="xo_stage")
         first_stage = keep.tile([P, 2, 2 * R // 4], I32, name="first_stage")
-        for stage, scales, cols in (
-            (xo_stage, xo_scales, slice(0, Z // 4)),
-            (first_stage, w_scales, slice(0, R // 4)),
-            (first_stage, w2_scales, slice(R // 4, 2 * R // 4)),
-        ):
+        def load_stage(queues, stage, scales, cols):
             for half in range(2):
-                (nc.sync, nc.scalar)[half].dma_start(
+                queues[half].dma_start(
                     stage[2 * QUAD * half : 2 * QUAD * half + PACK, :, cols],
                     staged_rows(scales)[:, 2 * half : 2 * half + 2, :],
                 )
+
+        load_stage((nc.sync, nc.scalar), first_stage, w_scales, slice(0, R // 4))
+        load_stage((nc.sync, nc.scalar), first_stage, w2_scales, slice(R // 4, 2 * R // 4))
         nc.scalar.dma_start(gs_sb[:], gs.rearrange("(p t) o -> p (t o)", t=PACK))
+        l1 = load_list("l1", offs)
         for t in range(2):
             nc.sync.dma_start(cq_sb[t][:], cq_rows[:, t, :])
+        load_stage((nc.sync, nc.sync), xo_stage, xo_scales, slice(0, Z // 4))
         l2 = load_list("l2", offs2)
-        l1 = load_list("l1", offs)
         for t in range(2, PACK):
             nc.sync.dma_start(cq_sb[t][:], cq_rows[:, t, :])
         xo_w = load_words("xo_w", xo_words[0], U16, Z)
@@ -83,12 +83,16 @@ def tile_list_leadsum_codednote_further_pagetwice_kernel(
         l3 = load_list("l3", offs3)
         l5 = load_list("l5", offs5)
         l4 = load_list("l4", offs4)
-        nc.sync.dma_start(second_stage[0:PACK, :, 0 : N // 4], staged_rows(wb_scales))
-        nc.sync.dma_start(second_stage[0:PACK, :, N // 4 : 2 * N // 4], staged_rows(ws_scales))
-        nc.sync.dma_start(second_stage[0:PACK, :, 2 * N // 4 :], staged_rows(sx_scales))
         wb_w = load_words("wb_w", wb_words[0].rearrange("p n t -> p (n t)"), U32, N)
         ws_w = load_words("ws_w", ws_words[0].rearrange("p n t -> p (n t)"), U32, N)
         sx_w = load_words("sx_w", sx_words[0], U16, O)
+        for scales, first_col in ((wb_scales, 0), (ws_scales, N), (sx_scales, 2 * N)):
+            width = scales.shape[2]
+            for q in range(PACK):
+                nc.sync.dma_start(
+                    second_plane[QUAD * q : QUAD * q + PACK, first_col : first_col + width].bitcast(I32),
+                    scales[0, PACK * q : PACK * (q + 1), :].bitcast(I32),
+                )
         l6 = load_list("l6", offs6)
         l7 = load_list("l7", offs7)
 
@@ -97,10 +101,10 @@ def tile_list_leadsum_codednote_further_pagetwice_kernel(
                 src = 2 * QUAD * (q // 2)
                 nc.vector.tensor_copy(plane[QUAD * q : QUAD * q + PACK].bitcast(I32), stage[src : src + PACK, q % 2, :])
 
-        spread(xo_plane, xo_stage)
         spread(first_plane_raw, first_stage)
         first_plane = keep.tile([P, 2, PACK, P], U8, name="first_plane", align_bytes=64)
         nc.vector.tensor_copy(first_plane[:], first_plane_raw[:].rearrange("p (i m t) -> p i t m", i=2, t=PACK))
+        spread(xo_plane, xo_stage)
         xo_pick_s = keep.tile([P, J], U8, name="xo_pick_s", align_bytes=64)
         nc.vector.tensor_copy(xo_pick_s[:], xo_plane[:].indirect(l2[:]))
 
@@ -131,34 +135,31 @@ def tile_list_leadsum_codednote_further_pagetwice_kernel(
         w2_w = [w2_first[:]] + [w2_rest[:, t, :] for t in range(PACK - 1)]
         w_w = [w_first[:]] + [w_rest[:, t, :] for t in range(PACK - 1)]
 
-        p_ps = [psum.tile([P, O], F32, name="p_ps%d" % h) for h in range(N // P)]
 
         picks = keep.tile([P, 3, PACK, O], F32, name="picks")
         part = keep.tile([P, PACK, O], F32, name="part")
         total = keep.tile([P, PACK - 1, O], F32, name="total")
-        total_last = keep.tile([P, O], F32, name="total_last")
+        total_last = keep.tile([P, 1, O], F32, name="total_last")
         a_sb, b_sb = [], []
         for t in range(PACK):
-            b_ps = psum.tile([P, J], F32, name="b_ps", tag="ab", bufs=6)
+            b_ps = psum.tile([P, J], F32, name="b_ps%d" % t, tag="bank%d" % (2 * t))
             nc.tensor.matmul_mx(
                 b_ps[:], lhsT=w2_w[t].bitcast(E5M2), lhsT_scale=first_plane[:, 1, t, :],
                 rhs=xo_pick_w[:].bitcast(E2M1), rhs_scale=xo_pick_s[:], start=True, stop=True,
             )
-            a_ps = psum.tile([P, J], F32, name="a_ps", tag="ab", bufs=6)
+            a_ps = psum.tile([P, J], F32, name="a_ps%d" % t, tag="bank%d" % (2 * t + 1))
             nc.tensor.matmul_mx(
                 a_ps[:], lhsT=w_w[t].bitcast(E2M1), lhsT_scale=first_plane[:, 0, t, :],
                 rhs=x1_codes[:].bitcast(E4M3), rhs_scale=x1_plane[:], start=True, stop=True,
             )
             b_t = keep.tile([P, J], F32, name="b%d" % t)
             a_t = keep.tile([P, J], F32, name="a%d" % t)
-            nc.vector.tensor_copy(b_t[:], b_ps[:])
+            (nc.scalar.copy if t == 0 else nc.vector.tensor_copy)(b_t[:], b_ps[:])
             nc.vector.tensor_copy(a_t[:], a_ps[:])
             a_sb.append(a_t)
             b_sb.append(b_t)
 
-        second_plane = keep.tile([P, 2 * N + O], U8, name="second_plane", tag="xo_w", align_bytes=64)
-        for q in range(PACK):
-            nc.vector.tensor_copy(second_plane[QUAD * q : QUAD * (q + 1)].bitcast(I32), second_stage[:, q, :])
+        p_ps = [psum.tile([P, O], F32, name="p_ps%d" % h, tag="bank%d" % (6 + h)) for h in range(N // P)]
         for h in range(N // P):
             nc.tensor.matmul_mx(
                 p_ps[h][:],
@@ -174,8 +175,12 @@ def tile_list_leadsum_codednote_further_pagetwice_kernel(
             nc.scalar.activation(picks[:, 0, t, :], a_sb[t][:].indirect(l3[:]), COPY, scale=b_sb[t][:, 0:1])
             nc.scalar.activation(picks[:, 1, t, :], a_sb[t][:].indirect(l5[:]), COPY, scale=b_sb[t][:, 128:129])
             nc.scalar.activation(picks[:, 2, t, :], b_sb[t][:].indirect(l4[:]), COPY, scale=a_sb[t][:, 0:1])
-            nc.vector.tensor_tensor(part[:, t, :], picks[:, 0, t, :], picks[:, 1, t, :], ADD)
-            nc.vector.tensor_tensor(total[:, t, :] if t < PACK - 1 else total_last[:], part[:, t, :], picks[:, 2, t, :], ADD)
+            if t > 0:
+                rows = slice(0 if t == 1 else t, t + 1)
+                nc.vector.tensor_tensor(part[:, rows, :], picks[:, 0, rows, :], picks[:, 1, rows, :], ADD)
+                nc.vector.tensor_tensor(
+                    total[:, rows, :] if t < PACK - 1 else total_last[:], part[:, rows, :], picks[:, 2, rows, :], ADD
+                )
 
         page_tags = (("x1_grouped", "w2_raw"), ("w_raw", "x1_late"))
         pages = [
@@ -190,7 +195,7 @@ def tile_list_leadsum_codednote_further_pagetwice_kernel(
         nc.vector.tensor_scalar(
             hid_grouped[:, :, 0 : PACK - 1], total[:, 0 : PACK - 1, :].rearrange("p t o -> p o t"), 0.0, None, MAX
         )
-        nc.vector.tensor_scalar(hid_grouped[:, :, PACK - 1], total_last[:], 0.0, None, MAX)
+        nc.vector.tensor_scalar(hid_grouped[:, :, PACK - 1], total_last[:, 0, :], 0.0, None, MAX)
         hid_codes = keep.tile([P, O], U32, name="hid_codes", align_bytes=64)
         hid_plane = keep.tile([P, O], U8, name="hid_plane", align_bytes=64)
         nc.vector.quantize_mx(hid_codes[:].bitcast(E4M3), hid_plane[:], hid_grouped[:].rearrange("p o t -> p (o t)"))
@@ -212,11 +217,10 @@ def tile_list_leadsum_codednote_further_pagetwice_kernel(
             nc.sync.dma_start(out[P * h : P * (h + 1), cols], both[:])
 
         for h, empty_bank in enumerate((nc.vector.tensor_copy, nc.scalar.copy)):
-            p_sb = keep.tile([P, O], F32, name="p%d" % h, tag="p_sb")
+            p_sb = keep.tile([P, O], F32, name="p%d" % h)
             empty_bank(p_sb[:], p_ps[h][:])
             nc.vector.tensor_copy(pages[h][0][:].indirect(l6[:]), p_sb[:])
             nc.scalar.activation(pages[h][1][:].indirect(l7[:]), p_sb[:], COPY)
-            if h == 0:
-                add_and_store(0, slice(0, E))
+        add_and_store(0, slice(0, E))
         add_and_store(1, slice(0, E // 2))
         add_and_store(1, slice(E // 2, E))

@@ -21,10 +21,10 @@ MAX = mybir.AluOpType.max
 P = 128
 PACK = 4
 QUAD = 32
-
-
-def staged_rows(scales):
-    return scales[0].bitcast(I32).rearrange("(q r) c -> r q c", r=PACK)
+WORD = 4
+SECOND_LEAD = 128
+VECTOR_COLUMNS = 176
+FIRST_STAGE_BANKS = 6
 
 
 def tile_list_leadsum_codednote_further_pagetwice_kernel(
@@ -36,6 +36,7 @@ def tile_list_leadsum_codednote_further_pagetwice_kernel(
         keep = ctx.enter_context(tc.tile_pool(name="keep", bufs=1))
         shared = ctx.enter_context(tc.tile_pool(name="shared", bufs=1))
         psum = ctx.enter_context(tc.psum_pool(name="psum", bufs=1))
+
 
         def load_list(name, src):
             tile = keep.tile(list(src.shape), U16, name=name)
@@ -58,22 +59,23 @@ def tile_list_leadsum_codednote_further_pagetwice_kernel(
         cq_sb = [keep.tile([P, T], F32, name="cq%d" % t) for t in range(PACK - 1)]
         cq_sb.append(shared.tile([P, T], F32, name="cq_last", offset=0, align_bytes=64))
         gs_sb = keep.tile([P, PACK], F32, name="gs_sb")
-        xo_stage = keep.tile([P, 2, Z // 4], I32, name="xo_stage")
-        first_stage = keep.tile([P, 2, 2 * R // 4], I32, name="first_stage")
+        xo_stage = keep.tile([P, 2, Z // WORD], I32, name="xo_stage")
+        first_stage = keep.tile([P, 2, 2 * R // WORD], I32, name="first_stage")
+
         def load_stage(queues, stage, scales, cols):
+            rows = scales[0].bitcast(I32).rearrange("(q s) c -> s q c", s=PACK)
             for half in range(2):
                 queues[half].dma_start(
-                    stage[2 * QUAD * half : 2 * QUAD * half + PACK, :, cols],
-                    staged_rows(scales)[:, 2 * half : 2 * half + 2, :],
+                    stage[2 * QUAD * half : 2 * QUAD * half + PACK, :, cols], rows[:, 2 * half : 2 * half + 2, :]
                 )
 
-        load_stage((nc.sync, nc.scalar), first_stage, w_scales, slice(0, R // 4))
-        load_stage((nc.sync, nc.scalar), first_stage, w2_scales, slice(R // 4, 2 * R // 4))
+        load_stage((nc.sync, nc.scalar), first_stage, w_scales, slice(0, R // WORD))
+        load_stage((nc.sync, nc.scalar), first_stage, w2_scales, slice(R // WORD, 2 * R // WORD))
         nc.scalar.dma_start(gs_sb[:], gs.rearrange("(p t) o -> p (t o)", t=PACK))
         l1 = load_list("l1", offs)
         for t in range(2):
             nc.sync.dma_start(cq_sb[t][:], cq_rows[:, t, :])
-        load_stage((nc.sync, nc.sync), xo_stage, xo_scales, slice(0, Z // 4))
+        load_stage((nc.sync, nc.sync), xo_stage, xo_scales, slice(0, Z // WORD))
         l2 = load_list("l2", offs2)
         for t in range(2, PACK):
             nc.sync.dma_start(cq_sb[t][:], cq_rows[:, t, :])
@@ -115,7 +117,9 @@ def tile_list_leadsum_codednote_further_pagetwice_kernel(
             row = x1_early[:, t, :] if t < 2 else x1_late[:, t - 2, :]
             nc.scalar.activation(row, cq_sb[t][:].indirect(l1[:]), COPY, scale=gs_sb[:, t : t + 1])
         nc.vector.tensor_copy(x1_grouped[:, :, 0:2], x1_early[:].rearrange("p t j -> p j t"))
-        nc.vector.tensor_copy(x1_grouped[:, :, 2:4], x1_late[:].rearrange("p t j -> p j t"))
+        late_pairs = x1_late[:].rearrange("p t j -> p j t")
+        nc.vector.tensor_copy(x1_grouped[:, 0:VECTOR_COLUMNS, 2:4], late_pairs[:, 0:VECTOR_COLUMNS, :])
+        nc.scalar.copy(x1_grouped[:, VECTOR_COLUMNS:, 2:4], late_pairs[:, VECTOR_COLUMNS:, :])
         xo_pick_w = keep.tile([P, J], U16, name="xo_pick_w", tag="x1_late", align_bytes=64)
         nc.vector.tensor_copy(xo_pick_w[:], xo_w[:].indirect(l2[:]))
         x1_codes = keep.tile([P, J], U32, name="x1_codes", tag="xo_w", align_bytes=64)
@@ -124,30 +128,30 @@ def tile_list_leadsum_codednote_further_pagetwice_kernel(
 
         w2_first = shared.tile([P, P], U32, name="w2_first", offset=0, align_bytes=64)
         w_first = shared.tile([P, P], U16, name="w_first", offset=4 * P, align_bytes=64)
-        w2_rest = shared.tile([P, PACK - 1, P], U32, name="w2_rest", offset=6 * P, align_bytes=64)
-        w_rest = shared.tile([P, PACK - 1, P], U16, name="w_rest", offset=18 * P, align_bytes=64)
+        w2_rest = shared.tile([P, PACK - 1, P], U32, name="w2_rest", offset=(4 + 2) * P, align_bytes=64)
+        w_rest = shared.tile([P, PACK - 1, P], U16, name="w_rest", offset=(4 * PACK + 2) * P, align_bytes=64)
         w2_cols = w2_raw[:].rearrange("p (m t) -> p m t", t=PACK)
         w_cols = w_raw[:].rearrange("p (m t) -> p t m", t=PACK)
         nc.scalar.copy(w2_first[:], w2_cols[:, :, 0])
         nc.scalar.copy(w_first[:], w_cols[:, 0, :])
-        nc.scalar.copy(w2_rest[:].rearrange("p t m -> p m t"), w2_cols[:, :, 1:])
         nc.scalar.copy(w_rest[:], w_cols[:, 1:, :])
+        nc.scalar.copy(w2_rest[:].rearrange("p t m -> p m t"), w2_cols[:, :, 1:])
         w2_w = [w2_first[:]] + [w2_rest[:, t, :] for t in range(PACK - 1)]
         w_w = [w_first[:]] + [w_rest[:, t, :] for t in range(PACK - 1)]
 
-
+        p_ps = [psum.tile([P, O], F32, name="p_ps%d" % h) for h in range(N // P)]
         picks = keep.tile([P, 3, PACK, O], F32, name="picks")
         part = keep.tile([P, PACK, O], F32, name="part")
-        total = keep.tile([P, PACK - 1, O], F32, name="total")
-        total_last = keep.tile([P, 1, O], F32, name="total_last")
+        total = keep.tile([P, PACK, O], F32, name="total")
+        hid_grouped = keep.tile([P, O, PACK], BF16, name="hid_grouped", align_bytes=64)
         a_sb, b_sb = [], []
         for t in range(PACK):
-            b_ps = psum.tile([P, J], F32, name="b_ps%d" % t, tag="bank%d" % (2 * t))
+            b_ps = psum.tile([P, J], F32, name="b_ps", tag="first", bufs=FIRST_STAGE_BANKS)
             nc.tensor.matmul_mx(
                 b_ps[:], lhsT=w2_w[t].bitcast(E5M2), lhsT_scale=first_plane[:, 1, t, :],
                 rhs=xo_pick_w[:].bitcast(E2M1), rhs_scale=xo_pick_s[:], start=True, stop=True,
             )
-            a_ps = psum.tile([P, J], F32, name="a_ps%d" % t, tag="bank%d" % (2 * t + 1))
+            a_ps = psum.tile([P, J], F32, name="a_ps", tag="first", bufs=FIRST_STAGE_BANKS)
             nc.tensor.matmul_mx(
                 a_ps[:], lhsT=w_w[t].bitcast(E2M1), lhsT_scale=first_plane[:, 0, t, :],
                 rhs=x1_codes[:].bitcast(E4M3), rhs_scale=x1_plane[:], start=True, stop=True,
@@ -159,27 +163,26 @@ def tile_list_leadsum_codednote_further_pagetwice_kernel(
             a_sb.append(a_t)
             b_sb.append(b_t)
 
-        p_ps = [psum.tile([P, O], F32, name="p_ps%d" % h, tag="bank%d" % (6 + h)) for h in range(N // P)]
         for h in range(N // P):
             nc.tensor.matmul_mx(
-                p_ps[h][:],
-                lhsT=ws_w[:, P * h : P * (h + 1)].bitcast(E5M2),
+                p_ps[h][:], lhsT=ws_w[:, P * h : P * (h + 1)].bitcast(E5M2),
                 lhsT_scale=second_plane[:, N + P * h : N + P * (h + 1)],
-                rhs=sx_w[:].bitcast(E2M1),
-                rhs_scale=second_plane[:, 2 * N :],
-                start=True,
-                stop=False,
+                rhs=sx_w[:].bitcast(E2M1), rhs_scale=second_plane[:, 2 * N :], start=True, stop=False,
             )
 
         for t in range(PACK):
-            nc.scalar.activation(picks[:, 0, t, :], a_sb[t][:].indirect(l3[:]), COPY, scale=b_sb[t][:, 0:1])
-            nc.scalar.activation(picks[:, 1, t, :], a_sb[t][:].indirect(l5[:]), COPY, scale=b_sb[t][:, 128:129])
-            nc.scalar.activation(picks[:, 2, t, :], b_sb[t][:].indirect(l4[:]), COPY, scale=a_sb[t][:, 0:1])
+            lead_b, lead_b2, lead_a = b_sb[t][:, 0:1], b_sb[t][:, SECOND_LEAD : SECOND_LEAD + 1], a_sb[t][:, 0:1]
+            nc.scalar.activation(picks[:, 0, t, :], a_sb[t][:].indirect(l3[:]), COPY, scale=lead_b)
+            nc.scalar.activation(picks[:, 1, t, :], a_sb[t][:].indirect(l5[:]), COPY, scale=lead_b2)
+            nc.scalar.activation(picks[:, 2, t, :], b_sb[t][:].indirect(l4[:]), COPY, scale=lead_a)
             if t > 0:
-                rows = slice(0 if t == 1 else t, t + 1)
-                nc.vector.tensor_tensor(part[:, rows, :], picks[:, 0, rows, :], picks[:, 1, rows, :], ADD)
-                nc.vector.tensor_tensor(
-                    total[:, rows, :] if t < PACK - 1 else total_last[:], part[:, rows, :], picks[:, 2, rows, :], ADD
+                slices = slice(0 if t == 1 else t, t + 1)
+                nc.vector.tensor_tensor(part[:, slices, :], picks[:, 0, slices, :], picks[:, 1, slices, :], ADD)
+                nc.vector.tensor_tensor(total[:, slices, :], part[:, slices, :], picks[:, 2, slices, :], ADD)
+            if t % 2 == 1:
+                pair = slice(t - 1, t + 1)
+                nc.vector.tensor_scalar(
+                    hid_grouped[:, :, pair], total[:, pair, :].rearrange("p t o -> p o t"), 0.0, None, MAX
                 )
 
         page_tags = (("x1_grouped", "w2_raw"), ("w_raw", "x1_late"))
@@ -191,36 +194,23 @@ def tile_list_leadsum_codednote_further_pagetwice_kernel(
             for s in range(2):
                 nc.gpsimd.memset(pages[h][s][:], 0.0)
 
-        hid_grouped = keep.tile([P, O, PACK], BF16, name="hid_grouped", align_bytes=64)
-        nc.vector.tensor_scalar(
-            hid_grouped[:, :, 0 : PACK - 1], total[:, 0 : PACK - 1, :].rearrange("p t o -> p o t"), 0.0, None, MAX
-        )
-        nc.vector.tensor_scalar(hid_grouped[:, :, PACK - 1], total_last[:, 0, :], 0.0, None, MAX)
         hid_codes = keep.tile([P, O], U32, name="hid_codes", align_bytes=64)
         hid_plane = keep.tile([P, O], U8, name="hid_plane", align_bytes=64)
         nc.vector.quantize_mx(hid_codes[:].bitcast(E4M3), hid_plane[:], hid_grouped[:].rearrange("p o t -> p (o t)"))
 
         for h in range(N // P):
             nc.tensor.matmul_mx(
-                p_ps[h][:],
-                lhsT=wb_w[:, P * h : P * (h + 1)].bitcast(E5M2),
+                p_ps[h][:], lhsT=wb_w[:, P * h : P * (h + 1)].bitcast(E5M2),
                 lhsT_scale=second_plane[:, P * h : P * (h + 1)],
-                rhs=hid_codes[:].bitcast(E4M3),
-                rhs_scale=hid_plane[:],
-                start=False,
-                stop=True,
+                rhs=hid_codes[:].bitcast(E4M3), rhs_scale=hid_plane[:], start=False, stop=True,
             )
-
-        def add_and_store(h, cols):
-            both = keep.tile([P, cols.stop - cols.start], F32, name="both%d_%d" % (h, cols.start))
-            nc.vector.tensor_tensor(both[:], pages[h][0][:, cols], pages[h][1][:, cols], ADD)
-            nc.sync.dma_start(out[P * h : P * (h + 1), cols], both[:])
 
         for h, empty_bank in enumerate((nc.vector.tensor_copy, nc.scalar.copy)):
             p_sb = keep.tile([P, O], F32, name="p%d" % h)
             empty_bank(p_sb[:], p_ps[h][:])
             nc.vector.tensor_copy(pages[h][0][:].indirect(l6[:]), p_sb[:])
             nc.scalar.activation(pages[h][1][:].indirect(l7[:]), p_sb[:], COPY)
-        add_and_store(0, slice(0, E))
-        add_and_store(1, slice(0, E // 2))
-        add_and_store(1, slice(E // 2, E))
+        for h, cols in ((0, slice(0, E)), (1, slice(0, E // 2)), (1, slice(E // 2, E))):
+            both = keep.tile([P, cols.stop - cols.start], F32, name="both%d_%d" % (h, cols.start))
+            nc.vector.tensor_tensor(both[:], pages[h][0][:, cols], pages[h][1][:, cols], ADD)
+            nc.sync.dma_start(out[P * h : P * (h + 1), cols], both[:])

from contextlib import ExitStack

import concourse.mybir as mybir

K, T, J, R, F, Z, O, N, L, E = 512, 1024, 256, 512, 512, 1024, 128, 256, 512, 512
FLOPS = 2 * (K * R * J + F * R * J + R * N * O + L * N * O)

F32 = mybir.dt.float32
BF16 = mybir.dt.bfloat16
I32 = mybir.dt.int32
U32 = mybir.dt.uint32
U16 = mybir.dt.uint16
U8 = mybir.dt.uint8
E4M3 = mybir.dt.float8_e4m3fn_x4
E5M2 = mybir.dt.float8_e5m2_x4
E2M1 = mybir.dt.float4_e2m1fn_x4
COPY = mybir.ActivationFunctionType.Copy
ADD = mybir.AluOpType.add
MAX = mybir.AluOpType.max

P = 128
PACK = 4
QUAD = 32
WORD = 4
SECOND_LEAD = 128
VECTOR_COLUMNS = 176
FIRST_STAGE_BANKS = 6


def tile_list_leadsum_codednote_further_pagetwice_kernel(
    tc, xo_words, xo_scales, cq, gs, w_words, w_scales, w2_words, w2_scales, wb_words, wb_scales,
    sx_words, sx_scales, ws_words, ws_scales, offs, offs2, offs3, offs4, offs5, offs6, offs7, out,
):
    nc = tc.nc
    with ExitStack() as ctx:
        keep = ctx.enter_context(tc.tile_pool(name="keep", bufs=1))
        shared = ctx.enter_context(tc.tile_pool(name="shared", bufs=1))
        psum = ctx.enter_context(tc.psum_pool(name="psum", bufs=1))


        def load_list(name, src):
            tile = keep.tile(list(src.shape), U16, name=name)
            nc.sync.dma_start(tile[:], src)
            return tile

        def load_words(name, src, dtype, cols):
            tile = keep.tile([P, cols], dtype, name=name, tag=name, align_bytes=64)
            nc.sync.dma_start(tile[:].bitcast(I32), src.bitcast(I32))
            return tile

        xo_plane = keep.tile([P, Z], U8, name="xo_plane", tag="x1_grouped", align_bytes=64)
        nc.vector.memset(xo_plane[:].bitcast(I32), 0)
        first_plane_raw = keep.tile([P, 2 * R], U8, name="first_plane_raw", align_bytes=64)
        nc.vector.memset(first_plane_raw[:].bitcast(I32), 0)
        second_plane = keep.tile([P, 2 * N + O], U8, name="second_plane", align_bytes=64)
        nc.vector.memset(second_plane[:].bitcast(I32), 0)

        cq_rows = cq.rearrange("(p t) c -> p t c", t=PACK)
        cq_sb = [keep.tile([P, T], F32, name="cq%d" % t) for t in range(PACK - 1)]
        cq_sb.append(shared.tile([P, T], F32, name="cq_last", offset=0, align_bytes=64))
        gs_sb = keep.tile([P, PACK], F32, name="gs_sb")
        xo_stage = keep.tile([P, 2, Z // WORD], I32, name="xo_stage")
        first_stage = keep.tile([P, 2, 2 * R // WORD], I32, name="first_stage")

        def load_stage(queues, stage, scales, cols):
            rows = scales[0].bitcast(I32).rearrange("(q s) c -> s q c", s=PACK)
            for half in range(2):
                queues[half].dma_start(
                    stage[2 * QUAD * half : 2 * QUAD * half + PACK, :, cols], rows[:, 2 * half : 2 * half + 2, :]
                )

        load_stage((nc.sync, nc.scalar), first_stage, w_scales, slice(0, R // WORD))
        load_stage((nc.sync, nc.scalar), first_stage, w2_scales, slice(R // WORD, 2 * R // WORD))
        nc.scalar.dma_start(gs_sb[:], gs.rearrange("(p t) o -> p (t o)", t=PACK))
        l1 = load_list("l1", offs)
        for t in range(2):
            nc.sync.dma_start(cq_sb[t][:], cq_rows[:, t, :])
        load_stage((nc.sync, nc.sync), xo_stage, xo_scales, slice(0, Z // WORD))
        l2 = load_list("l2", offs2)
        for t in range(2, PACK):
            nc.sync.dma_start(cq_sb[t][:], cq_rows[:, t, :])
        xo_w = load_words("xo_w", xo_words[0], U16, Z)
        w2_raw = load_words("w2_raw", w2_words[0].rearrange("p n t -> p (n t)"), U32, R)
        w_raw = load_words("w_raw", w_words[0], U16, R)
        l3 = load_list("l3", offs3)
        l5 = load_list("l5", offs5)
        l4 = load_list("l4", offs4)
        wb_w = load_words("wb_w", wb_words[0].rearrange("p n t -> p (n t)"), U32, N)
        ws_w = load_words("ws_w", ws_words[0].rearrange("p n t -> p (n t)"), U32, N)
        sx_w = load_words("sx_w", sx_words[0], U16, O)
        for scales, first_col in ((wb_scales, 0), (ws_scales, N), (sx_scales, 2 * N)):
            width = scales.shape[2]
            for q in range(PACK):
                nc.sync.dma_start(
                    second_plane[QUAD * q : QUAD * q + PACK, first_col : first_col + width].bitcast(I32),
                    scales[0, PACK * q : PACK * (q + 1), :].bitcast(I32),
                )
        l6 = load_list("l6", offs6)
        l7 = load_list("l7", offs7)

        def spread(plane, stage):
            for q in range(PACK):
                src = 2 * QUAD * (q // 2)
                nc.vector.tensor_copy(plane[QUAD * q : QUAD * q + PACK].bitcast(I32), stage[src : src + PACK, q % 2, :])

        spread(first_plane_raw, first_stage)
        first_plane = keep.tile([P, 2, PACK, P], U8, name="first_plane", align_bytes=64)
        nc.vector.tensor_copy(first_plane[:], first_plane_raw[:].rearrange("p (i m t) -> p i t m", i=2, t=PACK))
        spread(xo_plane, xo_stage)
        xo_pick_s = keep.tile([P, J], U8, name="xo_pick_s", align_bytes=64)
        nc.vector.tensor_copy(xo_pick_s[:], xo_plane[:].indirect(l2[:]))

        x1_grouped = keep.tile([P, J, PACK], BF16, name="x1_grouped", tag="x1_grouped", align_bytes=64)
        x1_early = keep.tile([P, 2, J], BF16, name="x1_early")
        x1_late = keep.tile([P, 2, J], BF16, name="x1_late", tag="x1_late", align_bytes=64)
        for t in range(PACK):
            row = x1_early[:, t, :] if t < 2 else x1_late[:, t - 2, :]
            nc.scalar.activation(row, cq_sb[t][:].indirect(l1[:]), COPY, scale=gs_sb[:, t : t + 1])
        nc.vector.tensor_copy(x1_grouped[:, :, 0:2], x1_early[:].rearrange("p t j -> p j t"))
        late_pairs = x1_late[:].rearrange("p t j -> p j t")
        nc.vector.tensor_copy(x1_grouped[:, 0:VECTOR_COLUMNS, 2:4], late_pairs[:, 0:VECTOR_COLUMNS, :])
        nc.scalar.copy(x1_grouped[:, VECTOR_COLUMNS:, 2:4], late_pairs[:, VECTOR_COLUMNS:, :])
        xo_pick_w = keep.tile([P, J], U16, name="xo_pick_w", tag="x1_late", align_bytes=64)
        nc.vector.tensor_copy(xo_pick_w[:], xo_w[:].indirect(l2[:]))
        x1_codes = keep.tile([P, J], U32, name="x1_codes", tag="xo_w", align_bytes=64)
        x1_plane = keep.tile([P, J], U8, name="x1_plane", align_bytes=64)
        nc.vector.quantize_mx(x1_codes[:].bitcast(E4M3), x1_plane[:], x1_grouped[:].rearrange("p j t -> p (j t)"))

        w2_first = shared.tile([P, P], U32, name="w2_first", offset=0, align_bytes=64)
        w_first = shared.tile([P, P], U16, name="w_first", offset=4 * P, align_bytes=64)
        w2_rest = shared.tile([P, PACK - 1, P], U32, name="w2_rest", offset=(4 + 2) * P, align_bytes=64)
        w_rest = shared.tile([P, PACK - 1, P], U16, name="w_rest", offset=(4 * PACK + 2) * P, align_bytes=64)
        w2_cols = w2_raw[:].rearrange("p (m t) -> p m t", t=PACK)
        w_cols = w_raw[:].rearrange("p (m t) -> p t m", t=PACK)
        nc.scalar.copy(w2_first[:], w2_cols[:, :, 0])
        nc.scalar.copy(w_first[:], w_cols[:, 0, :])
        nc.scalar.copy(w_rest[:], w_cols[:, 1:, :])
        nc.scalar.copy(w2_rest[:].rearrange("p t m -> p m t"), w2_cols[:, :, 1:])
        w2_w = [w2_first[:]] + [w2_rest[:, t, :] for t in range(PACK - 1)]
        w_w = [w_first[:]] + [w_rest[:, t, :] for t in range(PACK - 1)]

        p_ps = [psum.tile([P, O], F32, name="p_ps%d" % h) for h in range(N // P)]
        picks = keep.tile([P, 3, PACK, O], F32, name="picks")
        part = keep.tile([P, PACK, O], F32, name="part")
        total = keep.tile([P, PACK, O], F32, name="total")
        hid_grouped = keep.tile([P, O, PACK], BF16, name="hid_grouped", align_bytes=64)
        a_sb, b_sb = [], []
        for t in range(PACK):
            b_ps = psum.tile([P, J], F32, name="b_ps", tag="first", bufs=FIRST_STAGE_BANKS)
            nc.tensor.matmul_mx(
                b_ps[:], lhsT=w2_w[t].bitcast(E5M2), lhsT_scale=first_plane[:, 1, t, :],
                rhs=xo_pick_w[:].bitcast(E2M1), rhs_scale=xo_pick_s[:], start=True, stop=True,
            )
            a_ps = psum.tile([P, J], F32, name="a_ps", tag="first", bufs=FIRST_STAGE_BANKS)
            nc.tensor.matmul_mx(
                a_ps[:], lhsT=w_w[t].bitcast(E2M1), lhsT_scale=first_plane[:, 0, t, :],
                rhs=x1_codes[:].bitcast(E4M3), rhs_scale=x1_plane[:], start=True, stop=True,
            )
            b_t = keep.tile([P, J], F32, name="b%d" % t)
            a_t = keep.tile([P, J], F32, name="a%d" % t)
            (nc.scalar.copy if t == 0 else nc.vector.tensor_copy)(b_t[:], b_ps[:])
            nc.vector.tensor_copy(a_t[:], a_ps[:])
            a_sb.append(a_t)
            b_sb.append(b_t)

        for h in range(N // P):
            nc.tensor.matmul_mx(
                p_ps[h][:], lhsT=ws_w[:, P * h : P * (h + 1)].bitcast(E5M2),
                lhsT_scale=second_plane[:, N + P * h : N + P * (h + 1)],
                rhs=sx_w[:].bitcast(E2M1), rhs_scale=second_plane[:, 2 * N :], start=True, stop=False,
            )

        for t in range(PACK):
            lead_b, lead_b2, lead_a = b_sb[t][:, 0:1], b_sb[t][:, SECOND_LEAD : SECOND_LEAD + 1], a_sb[t][:, 0:1]
            nc.scalar.activation(picks[:, 0, t, :], a_sb[t][:].indirect(l3[:]), COPY, scale=lead_b)
            nc.scalar.activation(picks[:, 1, t, :], a_sb[t][:].indirect(l5[:]), COPY, scale=lead_b2)
            nc.scalar.activation(picks[:, 2, t, :], b_sb[t][:].indirect(l4[:]), COPY, scale=lead_a)
            if t > 0:
                slices = slice(0 if t == 1 else t, t + 1)
                nc.vector.tensor_tensor(part[:, slices, :], picks[:, 0, slices, :], picks[:, 1, slices, :], ADD)
                nc.vector.tensor_tensor(total[:, slices, :], part[:, slices, :], picks[:, 2, slices, :], ADD)
            if t % 2 == 1:
                pair = slice(t - 1, t + 1)
                nc.vector.tensor_scalar(
                    hid_grouped[:, :, pair], total[:, pair, :].rearrange("p t o -> p o t"), 0.0, None, MAX
                )

        page_tags = (("x1_grouped", "w2_raw"), ("w_raw", "x1_late"))
        pages = [
            [keep.tile([P, E], F32, name="page%d%d" % (h, s), tag=page_tags[h][s], align_bytes=64) for s in range(2)]
            for h in range(N // P)
        ]
        for h in range(N // P):
            for s in range(2):
                nc.gpsimd.memset(pages[h][s][:], 0.0)

        hid_codes = keep.tile([P, O], U32, name="hid_codes", align_bytes=64)
        hid_plane = keep.tile([P, O], U8, name="hid_plane", align_bytes=64)
        nc.vector.quantize_mx(hid_codes[:].bitcast(E4M3), hid_plane[:], hid_grouped[:].rearrange("p o t -> p (o t)"))

        for h in range(N // P):
            nc.tensor.matmul_mx(
                p_ps[h][:], lhsT=wb_w[:, P * h : P * (h + 1)].bitcast(E5M2),
                lhsT_scale=second_plane[:, P * h : P * (h + 1)],
                rhs=hid_codes[:].bitcast(E4M3), rhs_scale=hid_plane[:], start=False, stop=True,
            )

        for h, empty_bank in enumerate((nc.vector.tensor_copy, nc.scalar.copy)):
            p_sb = keep.tile([P, O], F32, name="p%d" % h)
            empty_bank(p_sb[:], p_ps[h][:])
            nc.vector.tensor_copy(pages[h][0][:].indirect(l6[:]), p_sb[:])
            nc.scalar.activation(pages[h][1][:].indirect(l7[:]), p_sb[:], COPY)
        for h, cols in ((0, slice(0, E)), (1, slice(0, E // 2)), (1, slice(E // 2, E))):
            both = keep.tile([P, cols.stop - cols.start], F32, name="both%d_%d" % (h, cols.start))
            nc.vector.tensor_tensor(both[:], pages[h][0][:, cols], pages[h][1][:, cols], ADD)
            nc.sync.dma_start(out[P * h : P * (h + 1), cols], both[:])
